import numpy as np
import ml_dtypes


def mxq(x, axis, fmt="e4m3"):
    dtype, down = {"e4m3": (ml_dtypes.float8_e4m3fn, 7), "e5m2": (ml_dtypes.float8_e5m2, 14)}[fmt]
    v = np.moveaxis(np.asarray(x, np.float32).astype(ml_dtypes.bfloat16).astype(np.float64), axis, -1)
    blocks = v.reshape(v.shape[:-1] + (-1, 32))
    amax = np.abs(blocks).max(-1, keepdims=True)
    byte = np.maximum(np.where(amax > 0, np.frexp(amax)[1] - 1 + 127, 0) - down, 1)
    scale = np.exp2(byte - 127.0)
    codes = (blocks / scale).astype(np.float32).astype(dtype).astype(np.float64)
    return np.moveaxis((codes * scale).reshape(v.shape), -1, axis)


WIDE = False


def mx_kscale(k):
    if not WIDE:
        return np.ones(k)
    levels = np.array([10, -10, 5, -5, 0])
    if k % 512:
        return np.exp2(np.random.permutation(np.resize(levels, k // 32))).repeat(32)
    a = np.empty((k // 512, 16))
    for p in range(k // 512):
        a[p, :8] = np.random.permutation(np.resize(levels, 8))
        for g in range(8):
            far = levels[np.abs(levels - a[p, g]) >= 10]
            a[p, g + 8] = far[np.random.randint(len(far))]
    return np.exp2(a.ravel()).repeat(32)


def f64(x):
    return np.asarray(x).astype(np.float64)


def striped(idx):
    return np.tile(np.asarray(idx).reshape(-1, 16).T, (8, 1)).astype(np.uint16)


def unstriped(offs):
    return offs[:16].T.reshape(-1).astype(np.int64)


E2M1 = np.array([0.0, 0.5, 1.0, 1.5, 2.0, 3.0, 4.0, 6.0, -0.0, -0.5, -1.0, -1.5, -2.0, -3.0, -4.0, -6.0])


def pack_weight(w, fmt):
    k, n = w.shape
    w = f64(np.asarray(w, np.float32).astype(ml_dtypes.bfloat16)).reshape(k // 32, 32, n)
    amax = np.abs(w).max(1)
    if fmt == "e4m3":
        byte = np.frexp(amax)[1] - 1 + 127 - 7
    else:
        mant, ex = np.frexp(amax / 6.0)
        byte = np.where(mant > 0.5, ex, ex - 1) + 127
    byte = np.clip(np.where(amax > 0, byte, 1), 1, 254)
    scaled = (w * np.exp2(127.0 - byte)[:, None, :]).reshape(k, n).astype(np.float32)
    by_word = np.ascontiguousarray(scaled.reshape(k // 512, 128, 4, n).transpose(0, 1, 3, 2))
    if fmt == "e4m3":
        words = by_word.astype(ml_dtypes.float8_e4m3fn).view(np.uint8)
    else:
        c = by_word.astype(ml_dtypes.float4_e2m1fn).view(np.uint8) & 0xF
        words = (c[..., 0::2] | (c[..., 1::2] << 4)).reshape(k // 512, 128, 2 * n)
    return np.ascontiguousarray(words), np.ascontiguousarray(byte.astype(np.uint8).reshape(k // 512, 16, n))


def unpack_weight(words, scales, fmt):
    g, _, n = scales.shape
    words = np.ascontiguousarray(words).reshape(g, 128, n, -1)
    if fmt == "e4m3":
        vals = words.view(ml_dtypes.float8_e4m3fn).astype(np.float64)
    else:
        nib = np.empty((g, 128, n, 4), np.uint8)
        nib[..., 0::2] = words & 0xF
        nib[..., 1::2] = words >> 4
        vals = E2M1[nib]
    vals = vals * np.repeat(np.exp2(scales.astype(np.float64) - 127.0), 8, axis=1)[..., None]
    return vals.transpose(0, 1, 3, 2).reshape(g * 512, n)


K, T, J, I, N, M = 1024, 1024, 512, 512, 512, 512


def setup_inputs():
    n = np.random.standard_normal
    idx = np.random.permutation(T)[:J]
    idx2 = np.random.permutation(T)[:I]
    fk = mx_kscale(K)
    fn = mx_kscale(N)
    xtp = pack_weight(n((K, T)) / fk[:, None], "e4m3")
    wap = pack_weight(n((K, N)) * 1 / np.sqrt(K) * fk[:, None] * fn, "e2m1")
    wbp = pack_weight(n((K, N)) * 1 / np.sqrt(K) * fk[:, None] * fn, "e4m3")
    wmp = pack_weight(n((N, M)) * 1 / np.sqrt(N) / fn[:, None], "e2m1")
    return {
        "xt_words": xtp[0],
        "xt_scales": xtp[1],
        "wa_words": wap[0],
        "wa_scales": wap[1],
        "wb_words": wbp[0],
        "wb_scales": wbp[1],
        "res": (n((N, T)) * 0.5 * fn[:, None]).astype(np.float32),
        "wm_words": wmp[0],
        "wm_scales": wmp[1],
        "ga": (np.random.uniform(0.4, 1.2, (1, J))).astype(np.float32),
        "gb": (np.random.uniform(0.4, 1.2, (1, I))).astype(np.float32),
        "offs": striped(idx),
        "offs2": striped(idx2),
    }


def reference(xt_words, xt_scales, wa_words, wa_scales, wb_words, wb_scales, res, wm_words, wm_scales, ga, gb, offs, offs2):
    idx = unstriped(offs)
    idx2 = unstriped(offs2)
    xtu = unpack_weight(xt_words, xt_scales, "e4m3")
    wau = unpack_weight(wa_words, wa_scales, "e2m1")
    wbu = unpack_weight(wb_words, wb_scales, "e4m3")
    wmu = unpack_weight(wm_words, wm_scales, "e2m1")
    xtidxg = xtu[:, idx]
    p = wau.T @ xtidxg
    xtidx2g = xtu[:, idx2]
    q = wbu.T @ xtidx2g
    pw = p * f64(ga)
    qw = q * f64(gb)
    pg = np.zeros((N, T))
    pg[:, idx] = pw
    qg = np.zeros((N, T))
    qg[:, idx2] = qw
    h1 = np.maximum(pg + qg + f64(res), 0.0)
    h1q = mxq(h1, 0, "e4m3")
    y = wmu.T @ h1q
    return y

@@ -1,0 +1,257 @@
+from contextlib import ExitStack
+
+import concourse.mybir as mybir
+from concourse.masks import make_identity
+
+K, T, S, N, M = 1024, 1024, 512, 512, 512
+FLOPS = 2 * (2 * K * N * S) + 2 * N * M * T
+
+F32 = mybir.dt.float32
+BF16 = mybir.dt.bfloat16
+I32 = mybir.dt.int32
+U32 = mybir.dt.uint32
+U16 = mybir.dt.uint16
+U8 = mybir.dt.uint8
+FP8X4 = mybir.dt.float8_e4m3fn_x4
+FP4X4 = mybir.dt.float4_e2m1fn_x4
+ALU = mybir.AluOpType
+ACT = mybir.ActivationFunctionType
+
+P = 128
+PACK = 4
+PASSES = K // (P * PACK)
+QUADS = 4
+ROWS = 4
+SLOT_BLOCKS = S // P
+CHUNK = 256
+CHUNKS = T // CHUNK
+PAIR = 2
+
+
+def tile_moe_experts_then_shared_layer_kernel(
+    tc, xt_words, xt_scales, wa_words, wa_scales, wb_words, wb_scales, res, wm_words, wm_scales, ga, gb, offs, offs2, out
+):
+    nc = tc.nc
+    with ExitStack() as ctx:
+        keep = ctx.enter_context(tc.tile_pool(name="keep", bufs=1))
+        psum = ctx.enter_context(tc.psum_pool(name="psum", bufs=4))
+
+        def sbuf(name, shape, dtype):
+            return keep.tile(shape, dtype, name=name, align_bytes=64)
+
+        def zero_bytes(plane):
+            nc.vector.memset(plane[:].bitcast(I32), 0)
+
+        list_a = keep.tile([P, S // 16], U16, name="list_a")
+        list_b = keep.tile([P, S // 16], U16, name="list_b")
+        x_words = [sbuf("x_words%d" % z, [P, T], I32) for z in range(PASSES)]
+        x_scales = sbuf("x_scales", [P, T], U8)
+        wb_codes = [sbuf("wb_codes%d" % z, [P, N], I32) for z in range(PASSES)]
+        wb_planes = sbuf("wb_planes", [P, N], U8)
+        wa_codes = sbuf("wa_codes", [P, PASSES, 2 * N], U8)
+        wa_planes = sbuf("wa_planes", [P, PASSES, N], U8)
+        wm_codes = sbuf("wm_codes", [P, 2 * M], U8)
+        wm_plane = sbuf("wm_plane", [P, M], U8)
+        gate_a = sbuf("gate_a", [P, SLOT_BLOCKS], F32)
+        gate_b = sbuf("gate_b", [P, SLOT_BLOCKS], F32)
+        stream = sbuf("stream", [P, CHUNKS, PACK, CHUNK], F32)
+        xa_plane1 = sbuf("xa_plane1", [P, S], U8)
+        ident = sbuf("ident", [P, P], F32)
+        win_a = [sbuf("win_a%d" % i, [P, T], F32) for i in range(2)]
+        win_b = [sbuf("win_b%d" % i, [P, T], F32) for i in range(2)]
+
+        for plane in (x_scales, wb_planes, wa_planes, wm_plane, xa_plane1):
+            zero_bytes(plane)
+
+        def load_stacked(plane, scales):
+            for q in range(QUADS):
+                nc.sync.dma_start(
+                    out=plane[32 * q : 32 * q + PASSES * ROWS, :].bitcast(I32),
+                    in_=scales[:, ROWS * q : ROWS * (q + 1), :].bitcast(I32),
+                )
+
+        def words_of(packed, z):
+            return packed[z].rearrange("p c r -> p (c r)").bitcast(I32)
+
+        nc.sync.dma_start(list_b[:], offs2)
+        nc.sync.dma_start(out=x_words[0][:], in_=words_of(xt_words, 0))
+        load_stacked(x_scales, xt_scales)
+        nc.sync.dma_start(out=x_words[1][:], in_=words_of(xt_words, 1))
+        nc.sync.dma_start(out=wb_codes[0][:], in_=words_of(wb_words, 0))
+        load_stacked(wb_planes, wb_scales)
+        nc.sync.dma_start(list_a[:], offs)
+        nc.sync.dma_start(out=wb_codes[1][:], in_=words_of(wb_words, 1))
+        with nc.allow_non_contiguous_dma(reason="one gate value a partition"):
+            nc.sync.dma_start(out=gate_b[:], in_=gb[0].rearrange("(c p) -> p c", p=P))
+        nc.sync.dma_start(out=wa_codes[:].bitcast(I32), in_=wa_words.rearrange("z p b -> p z b").bitcast(I32))
+        for q in range(QUADS):
+            nc.sync.dma_start(
+                out=wa_planes[32 * q : 32 * q + ROWS, :, :].bitcast(I32),
+                in_=wa_scales[:, ROWS * q : ROWS * (q + 1), :].rearrange("z q n -> q z n").bitcast(I32),
+            )
+        with nc.allow_non_contiguous_dma(reason="one gate value a partition"):
+            nc.sync.dma_start(out=gate_a[:], in_=ga[0].rearrange("(c p) -> p c", p=P))
+        res_rows = res.rearrange("(p r) t -> p r t", r=PACK)
+        for c in range(CHUNKS):
+            nc.sync.dma_start(out=stream[:, c, :, :], in_=res_rows[:, :, c * CHUNK : (c + 1) * CHUNK])
+        nc.sync.dma_start(out=wm_codes[:].bitcast(I32), in_=wm_words[0].bitcast(I32))
+        for q in range(QUADS):
+            nc.sync.dma_start(
+                out=wm_plane[32 * q : 32 * q + ROWS, :].bitcast(I32),
+                in_=wm_scales[0, ROWS * q : ROWS * (q + 1), :].bitcast(I32),
+            )
+
+        make_identity(nc, ident[:])
+        for window in win_b:
+            nc.vector.memset(window[:], 0.0)
+        for window in win_a:
+            nc.gpsimd.memset(window[:], 0.0)
+
+        def gather(name, offsets):
+            planes = sbuf(name + "_planes", [P, S], U8)
+            nc.vector.tensor_copy(planes[:], x_scales[:].indirect(offsets[:]))
+            codes = []
+            for z in range(PASSES):
+                picked = sbuf(name + "_codes%d" % z, [P, S], U32)
+                nc.vector.tensor_copy(picked[:], x_words[z][:].bitcast(U32).indirect(offsets[:]))
+                codes.append(picked)
+            return codes, planes
+
+        xb_codes, xb_planes = gather("xb", list_b)
+        xa_codes, xa_planes = gather("xa", list_a)
+        for q in range(QUADS):
+            nc.scalar.dma_start(
+                out=xa_plane1[32 * q : 32 * q + ROWS, :].bitcast(I32),
+                in_=xa_planes[32 * q + ROWS : 32 * q + 2 * ROWS, :].bitcast(I32),
+            )
+
+        def expert(name, codes, token_plane, weights, weight_plane, gate):
+            sums = [psum.tile([P, N], F32, name="sums", tag="sums") for c in range(SLOT_BLOCKS)]
+            for z in range(PASSES):
+                for c in range(SLOT_BLOCKS):
+                    slots = slice(c * P, (c + 1) * P)
+                    nc.tensor.matmul_mx(
+                        out=sums[c][:],
+                        lhsT=codes[z][:, slots].bitcast(FP8X4),
+                        lhsT_scale=token_plane(z, slots),
+                        rhs=weights(z),
+                        rhs_scale=weight_plane(z),
+                        start=(z == 0),
+                        stop=(z == PASSES - 1),
+                    )
+            gated = [sbuf(name + "_gated%d" % c, [P, PACK, P], F32) for c in range(SLOT_BLOCKS)]
+            results = []
+
+            def leave(rows):
+                for c in range(SLOT_BLOCKS):
+                    nc.scalar.activation(
+                        out=gated[c][:, rows, :],
+                        in_=sums[c][:].rearrange("p (m r) -> p r m", r=PACK)[:, rows, :],
+                        func=ACT.Copy,
+                        scale=gate[:, c : c + 1],
+                    )
+
+            def turn(r):
+                turned = psum.tile([P, S], F32, name="turned", tag="turned")
+                for c in range(SLOT_BLOCKS):
+                    nc.tensor.transpose(turned[:, c * P : (c + 1) * P], gated[c][:, r, :], ident[:])
+                result = sbuf(name + "_result%d" % r, [P, S], F32)
+                nc.scalar.copy(out=result[:], in_=turned[:])
+                results.append(result)
+
+            leave(slice(0, 1))
+            turn(0)
+            leave(slice(1, PACK))
+            for r in range(1, PACK):
+                turn(r)
+            return results
+
+        qw = expert(
+            "qw", xb_codes, lambda z, slots: xb_planes[ROWS * z :, slots],
+            lambda z: wb_codes[z][:].bitcast(FP8X4), lambda z: wb_planes[ROWS * z :, :], gate_b,
+        )
+        pw = expert(
+            "pw", xa_codes, lambda z, slots: (xa_planes, xa_plane1)[z][:, slots],
+            lambda z: wa_codes[:, z, :].bitcast(FP4X4), lambda z: wa_planes[:, z, :], gate_a,
+        )
+
+        def scatter(window, offsets, values):
+            nc.vector.tensor_copy(window[:].indirect(offsets[:]), values[:])
+
+        def add_plane(r, window):
+            nc.gpsimd.tensor_tensor(
+                stream[:, :, r, :], stream[:, :, r, :], window[:].rearrange("p (c t) -> p c t", c=CHUNKS), ALU.add
+            )
+
+        for r in range(PACK):
+            scatter(win_b[r % 2], list_b, qw[r])
+            add_plane(r, win_b[r % 2])
+        for r in range(PACK):
+            scatter(win_a[r % 2], list_a, pw[r])
+            if r < PACK - 1:
+                add_plane(r, win_a[r % 2])
+        last = PACK - 1
+        last_window = win_a[last % 2]
+
+        hidden = [sbuf("hidden%d" % c, [P, CHUNK, PACK], BF16) for c in range(CHUNKS)]
+        h_codes = [sbuf("h_codes%d" % c, [P, CHUNK], U32) for c in range(CHUNKS)]
+        h_plane = [sbuf("h_plane%d" % c, [P, CHUNK], U8) for c in range(CHUNKS)]
+
+        def add_last(c):
+            nc.vector.tensor_tensor(
+                stream[:, c, last, :], last_window[:, c * CHUNK : (c + 1) * CHUNK], stream[:, c, last, :], ALU.add
+            )
+
+        def rectify(c):
+            source = stream[:, c, :, :].rearrange("p r t -> p t r")
+            if c == 1:
+                nc.scalar.activation(out=hidden[c][:], in_=source, func=ACT.Relu)
+            else:
+                nc.vector.tensor_scalar(hidden[c][:], source, 0.0, None, ALU.max)
+
+        def quantise(c):
+            nc.vector.quantize_mx(
+                out=h_codes[c][:].bitcast(FP8X4), scales=h_plane[c][:], in_=hidden[c][:].rearrange("p t r -> p (t r)")
+            )
+
+        out_rows = out.rearrange("(b p) t -> p b t", p=P)
+
+        def project(c):
+            for half in range(M // P // PAIR):
+                y = psum.tile([P, PAIR, CHUNK], F32, name="y", tag="sums")
+                for i in range(PAIR):
+                    b = half * PAIR + i
+                    nc.tensor.matmul_mx(
+                        out=y[:, i, :],
+                        lhsT=wm_codes[:, 2 * b * P : 2 * (b + 1) * P].bitcast(FP4X4),
+                        lhsT_scale=wm_plane[:, b * P : (b + 1) * P],
+                        rhs=h_codes[c][:].bitcast(FP8X4),
+                        rhs_scale=h_plane[c][:],
+                        start=True,
+                        stop=True,
+                    )
+                staged = sbuf("staged%d_%d" % (c, half), [P, PAIR, CHUNK], F32)
+                if c == CHUNKS - 1 and half == 1:
+                    nc.vector.tensor_copy(staged[:], y[:])
+                else:
+                    nc.scalar.copy(out=staged[:], in_=y[:])
+                nc.sync.dma_start(
+                    out=out_rows[:, half * PAIR : (half + 1) * PAIR, c * CHUNK : (c + 1) * CHUNK], in_=staged[:]
+                )
+
+        add_last(0)
+        add_last(1)
+        rectify(0)
+        rectify(1)
+        add_last(2)
+        quantise(0)
+        project(0)
+        add_last(3)
+        rectify(2)
+        quantise(1)
+        project(1)
+        rectify(3)
+        quantise(2)
+        project(2)
+        quantise(3)
+        project(3)

@@ -1,4 +1,5 @@
 from contextlib import ExitStack
+from itertools import product
 
 import concourse.mybir as mybir
 from concourse.masks import make_identity
@@ -60,7 +61,8 @@ def tile_moe_experts_then_shared_layer_kernel(
         win_a = [sbuf("win_a%d" % i, [P, T], F32) for i in range(2)]
         win_b = [sbuf("win_b%d" % i, [P, T], F32) for i in range(2)]
 
-        for plane in (x_scales, wb_planes, wa_planes, wm_plane, xa_plane1):
+        nc.gpsimd.memset(x_scales[:].bitcast(I32), 0)
+        for plane in (wb_planes, wa_planes, wm_plane, xa_plane1):
             zero_bytes(plane)
 
         def load_stacked(plane, scales):
@@ -74,8 +76,8 @@ def tile_moe_experts_then_shared_layer_kernel(
             return packed[z].rearrange("p c r -> p (c r)").bitcast(I32)
 
         nc.sync.dma_start(list_b[:], offs2)
-        nc.sync.dma_start(out=x_words[0][:], in_=words_of(xt_words, 0))
         load_stacked(x_scales, xt_scales)
+        nc.sync.dma_start(out=x_words[0][:], in_=words_of(xt_words, 0))
         nc.sync.dma_start(out=x_words[1][:], in_=words_of(xt_words, 1))
         nc.sync.dma_start(out=wb_codes[0][:], in_=words_of(wb_words, 0))
         load_stacked(wb_planes, wb_scales)
@@ -120,15 +122,15 @@ def tile_moe_experts_then_shared_layer_kernel(
         xb_codes, xb_planes = gather("xb", list_b)
         xa_codes, xa_planes = gather("xa", list_a)
         for q in range(QUADS):
-            nc.scalar.dma_start(
+            nc.sync.dma_start(
                 out=xa_plane1[32 * q : 32 * q + ROWS, :].bitcast(I32),
                 in_=xa_planes[32 * q + ROWS : 32 * q + 2 * ROWS, :].bitcast(I32),
             )
 
-        def expert(name, codes, token_plane, weights, weight_plane, gate):
+        def expert(name, codes, token_plane, weights, weight_plane, gate, early):
             sums = [psum.tile([P, N], F32, name="sums", tag="sums") for c in range(SLOT_BLOCKS)]
-            for z in range(PASSES):
-                for c in range(SLOT_BLOCKS):
+            for c0, z, c1 in product(range(0, SLOT_BLOCKS, 2), range(PASSES), range(2)):
+                for c in (c0 + c1,):
                     slots = slice(c * P, (c + 1) * P)
                     nc.tensor.matmul_mx(
                         out=sums[c][:],
@@ -140,10 +142,10 @@ def tile_moe_experts_then_shared_layer_kernel(
                         stop=(z == PASSES - 1),
                     )
             gated = [sbuf(name + "_gated%d" % c, [P, PACK, P], F32) for c in range(SLOT_BLOCKS)]
-            results = []
+            results = [sbuf(name + "_result%d" % r, [P, S], F32) for r in range(PACK)]
 
-            def leave(rows):
-                for c in range(SLOT_BLOCKS):
+            def leave(rows, blocks):
+                for c in blocks:
                     nc.scalar.activation(
                         out=gated[c][:, rows, :],
                         in_=sums[c][:].rearrange("p (m r) -> p r m", r=PACK)[:, rows, :],
@@ -151,28 +153,30 @@ def tile_moe_experts_then_shared_layer_kernel(
                         scale=gate[:, c : c + 1],
                     )
 
-            def turn(r):
-                turned = psum.tile([P, S], F32, name="turned", tag="turned")
-                for c in range(SLOT_BLOCKS):
-                    nc.tensor.transpose(turned[:, c * P : (c + 1) * P], gated[c][:, r, :], ident[:])
-                result = sbuf(name + "_result%d" % r, [P, S], F32)
-                nc.scalar.copy(out=result[:], in_=turned[:])
-                results.append(result)
+            def turn(r, blocks):
+                turned = psum.tile([P, len(blocks) * P], F32, name="turned", tag="turned")
+                for i, c in enumerate(blocks):
+                    nc.tensor.transpose(turned[:, i * P : (i + 1) * P], gated[c][:, r, :], ident[:])
+                nc.scalar.copy(out=results[r][:, blocks[0] * P : (blocks[-1] + 1) * P], in_=turned[:])
 
-            leave(slice(0, 1))
-            turn(0)
-            leave(slice(1, PACK))
-            for r in range(1, PACK):
-                turn(r)
+            if early:
+                for blocks in (range(0, 2), range(2, 4)):
+                    leave(slice(0, 1), blocks)
+                    turn(0, blocks)
+                leave(slice(1, PACK), range(SLOT_BLOCKS))
+            else:
+                leave(slice(0, PACK), range(SLOT_BLOCKS))
+            for r in range(1 if early else 0, PACK):
+                turn(r, range(SLOT_BLOCKS))
             return results
 
         qw = expert(
             "qw", xb_codes, lambda z, slots: xb_planes[ROWS * z :, slots],
-            lambda z: wb_codes[z][:].bitcast(FP8X4), lambda z: wb_planes[ROWS * z :, :], gate_b,
+            lambda z: wb_codes[z][:].bitcast(FP8X4), lambda z: wb_planes[ROWS * z :, :], gate_b, True,
         )
         pw = expert(
             "pw", xa_codes, lambda z, slots: (xa_planes, xa_plane1)[z][:, slots],
-            lambda z: wa_codes[:, z, :].bitcast(FP4X4), lambda z: wa_planes[:, z, :], gate_a,
+            lambda z: wa_codes[:, z, :].bitcast(FP4X4), lambda z: wa_planes[:, z, :], gate_a, False,
         )
 
         def scatter(window, offsets, values):
@@ -183,14 +187,21 @@ def tile_moe_experts_then_shared_layer_kernel(
                 stream[:, :, r, :], stream[:, :, r, :], window[:].rearrange("p (c t) -> p c t", c=CHUNKS), ALU.add
             )
 
-        for r in range(PACK):
+        last = PACK - 1
+        for half in range(2):
+            nc.vector.tensor_copy(
+                win_b[0][:].indirect(list_b[:, half * 16 : (half + 1) * 16]), qw[0][:, half * 256 : (half + 1) * 256]
+            )
+        add_plane(0, win_b[0])
+        for r in range(1, last):
             scatter(win_b[r % 2], list_b, qw[r])
             add_plane(r, win_b[r % 2])
-        for r in range(PACK):
+        for r in range(last):
             scatter(win_a[r % 2], list_a, pw[r])
-            if r < PACK - 1:
-                add_plane(r, win_a[r % 2])
-        last = PACK - 1
+            add_plane(r, win_a[r % 2])
+        scatter(win_b[last % 2], list_b, qw[last])
+        add_plane(last, win_b[last % 2])
+        scatter(win_a[last % 2], list_a, pw[last])
         last_window = win_a[last % 2]
 
         hidden = [sbuf("hidden%d" % c, [P, CHUNK, PACK], BF16) for c in range(CHUNKS)]
@@ -203,11 +214,12 @@ def tile_moe_experts_then_shared_layer_kernel(
             )
 
         def rectify(c):
-            source = stream[:, c, :, :].rearrange("p r t -> p t r")
+            source = stream[:, c, :, :].rearrange("p r (g i) -> p g r i", i=4)
+            woven = hidden[c][:].rearrange("p (g i) r -> p g r i", i=4)
             if c == 1:
-                nc.scalar.activation(out=hidden[c][:], in_=source, func=ACT.Relu)
+                nc.scalar.activation(out=woven, in_=source, func=ACT.Relu)
             else:
-                nc.vector.tensor_scalar(hidden[c][:], source, 0.0, None, ALU.max)
+                nc.vector.tensor_scalar(woven, source, 0.0, None, ALU.max)
 
         def quantise(c):
             nc.vector.quantize_mx(
@@ -218,7 +230,7 @@ def tile_moe_experts_then_shared_layer_kernel(
 
         def project(c):
             for half in range(M // P // PAIR):
-                y = psum.tile([P, PAIR, CHUNK], F32, name="y", tag="sums")
+                y = psum.tile([P, PAIR, CHUNK], F32, name="y", tag=("sums", "turned")[half])
                 for i in range(PAIR):
                     b = half * PAIR + i
                     nc.tensor.matmul_mx(
@@ -231,7 +243,7 @@ def tile_moe_experts_then_shared_layer_kernel(
                         stop=True,
                     )
                 staged = sbuf("staged%d_%d" % (c, half), [P, PAIR, CHUNK], F32)
-                if c == CHUNKS - 1 and half == 1:
+                if c >= CHUNKS - 2 and half == 1:
                     nc.vector.tensor_copy(staged[:], y[:])
                 else:
                     nc.scalar.copy(out=staged[:], in_=y[:])

@@ -41,7 +41,7 @@ def tile_moe_experts_then_shared_layer_kernel(
             return keep.tile(shape, dtype, name=name, align_bytes=64)
 
         def zero_bytes(plane):
-            nc.vector.memset(plane[:].bitcast(I32), 0)
+            nc.gpsimd.memset(plane[:].bitcast(I32), 0)
 
         list_a = keep.tile([P, S // 16], U16, name="list_a")
         list_b = keep.tile([P, S // 16], U16, name="list_b")
@@ -55,7 +55,7 @@ def tile_moe_experts_then_shared_layer_kernel(
         wm_plane = sbuf("wm_plane", [P, M], U8)
         gate_a = sbuf("gate_a", [P, SLOT_BLOCKS], F32)
         gate_b = sbuf("gate_b", [P, SLOT_BLOCKS], F32)
-        stream = sbuf("stream", [P, CHUNKS, PACK, CHUNK], F32)
+        stream = sbuf("stream", [P, PACK, T], F32)
         xa_plane1 = sbuf("xa_plane1", [P, S], U8)
         ident = sbuf("ident", [P, P], F32)
         win_a = [sbuf("win_a%d" % i, [P, T], F32) for i in range(2)]
@@ -94,8 +94,8 @@ def tile_moe_experts_then_shared_layer_kernel(
         with nc.allow_non_contiguous_dma(reason="one gate value a partition"):
             nc.sync.dma_start(out=gate_a[:], in_=ga[0].rearrange("(c p) -> p c", p=P))
         res_rows = res.rearrange("(p r) t -> p r t", r=PACK)
-        for c in range(CHUNKS):
-            nc.sync.dma_start(out=stream[:, c, :, :], in_=res_rows[:, :, c * CHUNK : (c + 1) * CHUNK])
+        for r in range(PACK):
+            nc.sync.dma_start(out=stream[:, r, :], in_=res_rows[:, r, :])
         nc.sync.dma_start(out=wm_codes[:].bitcast(I32), in_=wm_words[0].bitcast(I32))
         for q in range(QUADS):
             nc.sync.dma_start(
@@ -104,23 +104,30 @@ def tile_moe_experts_then_shared_layer_kernel(
             )
 
         make_identity(nc, ident[:])
+        primed = sbuf("primed", [P, 1], F32)
+        nc.scalar.activation(out=primed[:], in_=ident[:, :1], func=ACT.Copy)
         for window in win_b:
-            nc.vector.memset(window[:], 0.0)
+            nc.gpsimd.memset(window[:], 0.0)
         for window in win_a:
             nc.gpsimd.memset(window[:], 0.0)
 
-        def gather(name, offsets):
+        def gather_planes(name, offsets):
             planes = sbuf(name + "_planes", [P, S], U8)
             nc.vector.tensor_copy(planes[:], x_scales[:].indirect(offsets[:]))
+            return planes
+
+        def gather_codes(name, offsets):
             codes = []
             for z in range(PASSES):
                 picked = sbuf(name + "_codes%d" % z, [P, S], U32)
                 nc.vector.tensor_copy(picked[:], x_words[z][:].bitcast(U32).indirect(offsets[:]))
                 codes.append(picked)
-            return codes, planes
+            return codes
 
-        xb_codes, xb_planes = gather("xb", list_b)
-        xa_codes, xa_planes = gather("xa", list_a)
+        xb_planes = gather_planes("xb", list_b)
+        xb_codes = gather_codes("xb", list_b)
+        xa_planes = gather_planes("xa", list_a)
+        xa_codes = gather_codes("xa", list_a)
         for q in range(QUADS):
             nc.sync.dma_start(
                 out=xa_plane1[32 * q : 32 * q + ROWS, :].bitcast(I32),
@@ -163,10 +170,8 @@ def tile_moe_experts_then_shared_layer_kernel(
                 for blocks in (range(0, 2), range(2, 4)):
                     leave(slice(0, 1), blocks)
                     turn(0, blocks)
-                leave(slice(1, PACK), range(SLOT_BLOCKS))
-            else:
-                leave(slice(0, PACK), range(SLOT_BLOCKS))
             for r in range(1 if early else 0, PACK):
+                leave(slice(r, r + 1), range(SLOT_BLOCKS))
                 turn(r, range(SLOT_BLOCKS))
             return results
 
@@ -183,9 +188,7 @@ def tile_moe_experts_then_shared_layer_kernel(
             nc.vector.tensor_copy(window[:].indirect(offsets[:]), values[:])
 
         def add_plane(r, window):
-            nc.gpsimd.tensor_tensor(
-                stream[:, :, r, :], stream[:, :, r, :], window[:].rearrange("p (c t) -> p c t", c=CHUNKS), ALU.add
-            )
+            nc.gpsimd.tensor_tensor(stream[:, r, :], stream[:, r, :], window[:], ALU.add)
 
         last = PACK - 1
         for half in range(2):
@@ -193,15 +196,25 @@ def tile_moe_experts_then_shared_layer_kernel(
                 win_b[0][:].indirect(list_b[:, half * 16 : (half + 1) * 16]), qw[0][:, half * 256 : (half + 1) * 256]
             )
         add_plane(0, win_b[0])
-        for r in range(1, last):
+        for r in range(1, PACK):
             scatter(win_b[r % 2], list_b, qw[r])
             add_plane(r, win_b[r % 2])
         for r in range(last):
             scatter(win_a[r % 2], list_a, pw[r])
             add_plane(r, win_a[r % 2])
-        scatter(win_b[last % 2], list_b, qw[last])
-        add_plane(last, win_b[last % 2])
         scatter(win_a[last % 2], list_a, pw[last])
+        warm = psum.tile([P, N], F32, name="warm", tag="turned")
+        nc.tensor.transpose(warm[:, :P], stream[:, last - 1, :P], ident[:])
+        for b in range(4):
+            nc.tensor.matmul_mx(
+                out=warm[:],
+                lhsT=wm_codes[:, 2 * b * P : 2 * (b + 1) * P].bitcast(FP4X4),
+                lhsT_scale=wm_plane[:, b * P : (b + 1) * P],
+                rhs=wb_codes[0][:].bitcast(FP8X4),
+                rhs_scale=wb_planes[:],
+                start=True,
+                stop=True,
+            )
         last_window = win_a[last % 2]
 
         hidden = [sbuf("hidden%d" % c, [P, CHUNK, PACK], BF16) for c in range(CHUNKS)]
@@ -210,11 +223,14 @@ def tile_moe_experts_then_shared_layer_kernel(
 
         def add_last(c):
             nc.vector.tensor_tensor(
-                stream[:, c, last, :], last_window[:, c * CHUNK : (c + 1) * CHUNK], stream[:, c, last, :], ALU.add
+                stream[:, last, c * CHUNK : (c + 1) * CHUNK],
+                last_window[:, c * CHUNK : (c + 1) * CHUNK],
+                stream[:, last, c * CHUNK : (c + 1) * CHUNK],
+                ALU.add,
             )
 
         def rectify(c):
-            source = stream[:, c, :, :].rearrange("p r (g i) -> p g r i", i=4)
+            source = stream[:, :, c * CHUNK : (c + 1) * CHUNK].rearrange("p r (g i) -> p g r i", i=4)
             woven = hidden[c][:].rearrange("p (g i) r -> p g r i", i=4)
             if c == 1:
                 nc.scalar.activation(out=woven, in_=source, func=ACT.Relu)
@@ -255,13 +271,13 @@ def tile_moe_experts_then_shared_layer_kernel(
         add_last(1)
         rectify(0)
         rectify(1)
-        add_last(2)
         quantise(0)
         project(0)
+        add_last(2)
         add_last(3)
-        rectify(2)
         quantise(1)
         project(1)
+        rectify(2)
         rectify(3)
         quantise(2)
         project(2)

from contextlib import ExitStack
from itertools import product

import concourse.mybir as mybir
from concourse.masks import make_identity

K, T, S, N, M = 1024, 1024, 512, 512, 512
FLOPS = 2 * (2 * K * N * S) + 2 * N * M * T

F32 = mybir.dt.float32
BF16 = mybir.dt.bfloat16
I32 = mybir.dt.int32
U32 = mybir.dt.uint32
U16 = mybir.dt.uint16
U8 = mybir.dt.uint8
FP8X4 = mybir.dt.float8_e4m3fn_x4
FP4X4 = mybir.dt.float4_e2m1fn_x4
ALU = mybir.AluOpType
ACT = mybir.ActivationFunctionType

P = 128
PACK = 4
PASSES = K // (P * PACK)
QUADS = 4
ROWS = 4
SLOT_BLOCKS = S // P
CHUNK = 256
CHUNKS = T // CHUNK
PAIR = 2


def tile_moe_experts_then_shared_layer_kernel(
    tc, xt_words, xt_scales, wa_words, wa_scales, wb_words, wb_scales, res, wm_words, wm_scales, ga, gb, offs, offs2, out
):
    nc = tc.nc
    with ExitStack() as ctx:
        keep = ctx.enter_context(tc.tile_pool(name="keep", bufs=1))
        psum = ctx.enter_context(tc.psum_pool(name="psum", bufs=4))

        def sbuf(name, shape, dtype):
            return keep.tile(shape, dtype, name=name, align_bytes=64)

        def zero_bytes(plane):
            nc.gpsimd.memset(plane[:].bitcast(I32), 0)

        list_a = keep.tile([P, S // 16], U16, name="list_a")
        list_b = keep.tile([P, S // 16], U16, name="list_b")
        x_words = [sbuf("x_words%d" % z, [P, T], I32) for z in range(PASSES)]
        x_scales = sbuf("x_scales", [P, T], U8)
        wb_codes = [sbuf("wb_codes%d" % z, [P, N], I32) for z in range(PASSES)]
        wb_planes = sbuf("wb_planes", [P, N], U8)
        wa_codes = sbuf("wa_codes", [P, PASSES, 2 * N], U8)
        wa_planes = sbuf("wa_planes", [P, PASSES, N], U8)
        wm_codes = sbuf("wm_codes", [P, 2 * M], U8)
        wm_plane = sbuf("wm_plane", [P, M], U8)
        gate_a = sbuf("gate_a", [P, SLOT_BLOCKS], F32)
        gate_b = sbuf("gate_b", [P, SLOT_BLOCKS], F32)
        stream = sbuf("stream", [P, PACK, T], F32)
        xa_plane1 = sbuf("xa_plane1", [P, S], U8)
        ident = sbuf("ident", [P, P], F32)
        win_a = [sbuf("win_a%d" % i, [P, T], F32) for i in range(2)]
        win_b = [sbuf("win_b%d" % i, [P, T], F32) for i in range(2)]

        nc.gpsimd.memset(x_scales[:].bitcast(I32), 0)
        for plane in (wb_planes, wa_planes, wm_plane, xa_plane1):
            zero_bytes(plane)

        def load_stacked(plane, scales):
            for q in range(QUADS):
                nc.sync.dma_start(
                    out=plane[32 * q : 32 * q + PASSES * ROWS, :].bitcast(I32),
                    in_=scales[:, ROWS * q : ROWS * (q + 1), :].bitcast(I32),
                )

        def words_of(packed, z):
            return packed[z].rearrange("p c r -> p (c r)").bitcast(I32)

        nc.sync.dma_start(list_b[:], offs2)
        load_stacked(x_scales, xt_scales)
        nc.sync.dma_start(out=x_words[0][:], in_=words_of(xt_words, 0))
        nc.sync.dma_start(out=x_words[1][:], in_=words_of(xt_words, 1))
        nc.sync.dma_start(out=wb_codes[0][:], in_=words_of(wb_words, 0))
        load_stacked(wb_planes, wb_scales)
        nc.sync.dma_start(list_a[:], offs)
        nc.sync.dma_start(out=wb_codes[1][:], in_=words_of(wb_words, 1))
        with nc.allow_non_contiguous_dma(reason="one gate value a partition"):
            nc.sync.dma_start(out=gate_b[:], in_=gb[0].rearrange("(c p) -> p c", p=P))
        nc.sync.dma_start(out=wa_codes[:].bitcast(I32), in_=wa_words.rearrange("z p b -> p z b").bitcast(I32))
        for q in range(QUADS):
            nc.sync.dma_start(
                out=wa_planes[32 * q : 32 * q + ROWS, :, :].bitcast(I32),
                in_=wa_scales[:, ROWS * q : ROWS * (q + 1), :].rearrange("z q n -> q z n").bitcast(I32),
            )
        with nc.allow_non_contiguous_dma(reason="one gate value a partition"):
            nc.sync.dma_start(out=gate_a[:], in_=ga[0].rearrange("(c p) -> p c", p=P))
        res_rows = res.rearrange("(p r) t -> p r t", r=PACK)
        for r in range(PACK):
            nc.sync.dma_start(out=stream[:, r, :], in_=res_rows[:, r, :])
        nc.sync.dma_start(out=wm_codes[:].bitcast(I32), in_=wm_words[0].bitcast(I32))
        for q in range(QUADS):
            nc.sync.dma_start(
                out=wm_plane[32 * q : 32 * q + ROWS, :].bitcast(I32),
                in_=wm_scales[0, ROWS * q : ROWS * (q + 1), :].bitcast(I32),
            )

        make_identity(nc, ident[:])
        primed = sbuf("primed", [P, 1], F32)
        nc.scalar.activation(out=primed[:], in_=ident[:, :1], func=ACT.Copy)
        for window in win_b:
            nc.gpsimd.memset(window[:], 0.0)
        for window in win_a:
            nc.gpsimd.memset(window[:], 0.0)

        def gather_planes(name, offsets):
            planes = sbuf(name + "_planes", [P, S], U8)
            nc.vector.tensor_copy(planes[:], x_scales[:].indirect(offsets[:]))
            return planes

        def gather_codes(name, offsets):
            codes = []
            for z in range(PASSES):
                picked = sbuf(name + "_codes%d" % z, [P, S], U32)
                nc.vector.tensor_copy(picked[:], x_words[z][:].bitcast(U32).indirect(offsets[:]))
                codes.append(picked)
            return codes

        xb_planes = gather_planes("xb", list_b)
        xb_codes = gather_codes("xb", list_b)
        xa_planes = gather_planes("xa", list_a)
        xa_codes = gather_codes("xa", list_a)
        for q in range(QUADS):
            nc.sync.dma_start(
                out=xa_plane1[32 * q : 32 * q + ROWS, :].bitcast(I32),
                in_=xa_planes[32 * q + ROWS : 32 * q + 2 * ROWS, :].bitcast(I32),
            )

        def expert(name, codes, token_plane, weights, weight_plane, gate, early):
            sums = [psum.tile([P, N], F32, name="sums", tag="sums") for c in range(SLOT_BLOCKS)]
            for c0, z, c1 in product(range(0, SLOT_BLOCKS, 2), range(PASSES), range(2)):
                for c in (c0 + c1,):
                    slots = slice(c * P, (c + 1) * P)
                    nc.tensor.matmul_mx(
                        out=sums[c][:],
                        lhsT=codes[z][:, slots].bitcast(FP8X4),
                        lhsT_scale=token_plane(z, slots),
                        rhs=weights(z),
                        rhs_scale=weight_plane(z),
                        start=(z == 0),
                        stop=(z == PASSES - 1),
                    )
            gated = [sbuf(name + "_gated%d" % c, [P, PACK, P], F32) for c in range(SLOT_BLOCKS)]
            results = [sbuf(name + "_result%d" % r, [P, S], F32) for r in range(PACK)]

            def leave(rows, blocks):
                for c in blocks:
                    nc.scalar.activation(
                        out=gated[c][:, rows, :],
                        in_=sums[c][:].rearrange("p (m r) -> p r m", r=PACK)[:, rows, :],
                        func=ACT.Copy,
                        scale=gate[:, c : c + 1],
                    )

            def turn(r, blocks):
                turned = psum.tile([P, len(blocks) * P], F32, name="turned", tag="turned")
                for i, c in enumerate(blocks):
                    nc.tensor.transpose(turned[:, i * P : (i + 1) * P], gated[c][:, r, :], ident[:])
                nc.scalar.copy(out=results[r][:, blocks[0] * P : (blocks[-1] + 1) * P], in_=turned[:])

            if early:
                for blocks in (range(0, 2), range(2, 4)):
                    leave(slice(0, 1), blocks)
                    turn(0, blocks)
            for r in range(1 if early else 0, PACK):
                leave(slice(r, r + 1), range(SLOT_BLOCKS))
                turn(r, range(SLOT_BLOCKS))
            return results

        qw = expert(
            "qw", xb_codes, lambda z, slots: xb_planes[ROWS * z :, slots],
            lambda z: wb_codes[z][:].bitcast(FP8X4), lambda z: wb_planes[ROWS * z :, :], gate_b, True,
        )
        pw = expert(
            "pw", xa_codes, lambda z, slots: (xa_planes, xa_plane1)[z][:, slots],
            lambda z: wa_codes[:, z, :].bitcast(FP4X4), lambda z: wa_planes[:, z, :], gate_a, False,
        )

        def scatter(window, offsets, values):
            nc.vector.tensor_copy(window[:].indirect(offsets[:]), values[:])

        def add_plane(r, window):
            nc.gpsimd.tensor_tensor(stream[:, r, :], stream[:, r, :], window[:], ALU.add)

        last = PACK - 1
        for half in range(2):
            nc.vector.tensor_copy(
                win_b[0][:].indirect(list_b[:, half * 16 : (half + 1) * 16]), qw[0][:, half * 256 : (half + 1) * 256]
            )
        add_plane(0, win_b[0])
        for r in range(1, PACK):
            scatter(win_b[r % 2], list_b, qw[r])
            add_plane(r, win_b[r % 2])
        for r in range(last):
            scatter(win_a[r % 2], list_a, pw[r])
            add_plane(r, win_a[r % 2])
        scatter(win_a[last % 2], list_a, pw[last])
        warm = psum.tile([P, N], F32, name="warm", tag="turned")
        nc.tensor.transpose(warm[:, :P], stream[:, last - 1, :P], ident[:])
        for b in range(4):
            nc.tensor.matmul_mx(
                out=warm[:],
                lhsT=wm_codes[:, 2 * b * P : 2 * (b + 1) * P].bitcast(FP4X4),
                lhsT_scale=wm_plane[:, b * P : (b + 1) * P],
                rhs=wb_codes[0][:].bitcast(FP8X4),
                rhs_scale=wb_planes[:],
                start=True,
                stop=True,
            )
        last_window = win_a[last % 2]

        hidden = [sbuf("hidden%d" % c, [P, CHUNK, PACK], BF16) for c in range(CHUNKS)]
        h_codes = [sbuf("h_codes%d" % c, [P, CHUNK], U32) for c in range(CHUNKS)]
        h_plane = [sbuf("h_plane%d" % c, [P, CHUNK], U8) for c in range(CHUNKS)]

        def add_last(c):
            nc.vector.tensor_tensor(
                stream[:, last, c * CHUNK : (c + 1) * CHUNK],
                last_window[:, c * CHUNK : (c + 1) * CHUNK],
                stream[:, last, c * CHUNK : (c + 1) * CHUNK],
                ALU.add,
            )

        def rectify(c):
            source = stream[:, :, c * CHUNK : (c + 1) * CHUNK].rearrange("p r (g i) -> p g r i", i=4)
            woven = hidden[c][:].rearrange("p (g i) r -> p g r i", i=4)
            if c == 1:
                nc.scalar.activation(out=woven, in_=source, func=ACT.Relu)
            else:
                nc.vector.tensor_scalar(woven, source, 0.0, None, ALU.max)

        def quantise(c):
            nc.vector.quantize_mx(
                out=h_codes[c][:].bitcast(FP8X4), scales=h_plane[c][:], in_=hidden[c][:].rearrange("p t r -> p (t r)")
            )

        out_rows = out.rearrange("(b p) t -> p b t", p=P)

        def project(c):
            for half in range(M // P // PAIR):
                y = psum.tile([P, PAIR, CHUNK], F32, name="y", tag=("sums", "turned")[half])
                for i in range(PAIR):
                    b = half * PAIR + i
                    nc.tensor.matmul_mx(
                        out=y[:, i, :],
                        lhsT=wm_codes[:, 2 * b * P : 2 * (b + 1) * P].bitcast(FP4X4),
                        lhsT_scale=wm_plane[:, b * P : (b + 1) * P],
                        rhs=h_codes[c][:].bitcast(FP8X4),
                        rhs_scale=h_plane[c][:],
                        start=True,
                        stop=True,
                    )
                staged = sbuf("staged%d_%d" % (c, half), [P, PAIR, CHUNK], F32)
                if c >= CHUNKS - 2 and half == 1:
                    nc.vector.tensor_copy(staged[:], y[:])
                else:
                    nc.scalar.copy(out=staged[:], in_=y[:])
                nc.sync.dma_start(
                    out=out_rows[:, half * PAIR : (half + 1) * PAIR, c * CHUNK : (c + 1) * CHUNK], in_=staged[:]
                )

        add_last(0)
        add_last(1)
        rectify(0)
        rectify(1)
        quantise(0)
        project(0)
        add_last(2)
        add_last(3)
        quantise(1)
        project(1)
        rectify(2)
        rectify(3)
        quantise(2)
        project(2)
        quantise(3)
        project(3)
